import numpy as np
import ml_dtypes


def mxq(x, axis, fmt="e4m3"):
    dtype, down = {"e4m3": (ml_dtypes.float8_e4m3fn, 7), "e5m2": (ml_dtypes.float8_e5m2, 14)}[fmt]
    v = np.moveaxis(np.asarray(x, np.float32).astype(ml_dtypes.bfloat16).astype(np.float64), axis, -1)
    blocks = v.reshape(v.shape[:-1] + (-1, 32))
    amax = np.abs(blocks).max(-1, keepdims=True)
    byte = np.maximum(np.where(amax > 0, np.frexp(amax)[1] - 1 + 127, 0) - down, 1)
    scale = np.exp2(byte - 127.0)
    codes = (blocks / scale).astype(np.float32).astype(dtype).astype(np.float64)
    return np.moveaxis((codes * scale).reshape(v.shape), -1, axis)


WIDE = False


def mx_kscale(k):
    if not WIDE:
        return np.ones(k)
    levels = np.array([10, -10, 5, -5, 0])
    if k % 512:
        return np.exp2(np.random.permutation(np.resize(levels, k // 32))).repeat(32)
    a = np.empty((k // 512, 16))
    for p in range(k // 512):
        a[p, :8] = np.random.permutation(np.resize(levels, 8))
        for g in range(8):
            far = levels[np.abs(levels - a[p, g]) >= 10]
            a[p, g + 8] = far[np.random.randint(len(far))]
    return np.exp2(a.ravel()).repeat(32)


def f64(x):
    return np.asarray(x).astype(np.float64)


def striped(idx):
    return np.tile(idx.reshape(-1, 16).T, (8, 1)).astype(np.uint16)


def unstriped(offs):
    return offs[:16].T.reshape(-1).astype(np.int64)


def striped8(idx):
    return np.concatenate([x.reshape(-1, 16).T for x in idx]).astype(np.uint16)


def runs(offs, k):
    lists = np.stack([offs[16 * r : 16 * r + 16].T.reshape(-1) for r in range(8)]).astype(np.int64)
    return lists[np.arange(k) % 512 // 64]


def pack_weight(w):
    k, n = w.shape
    w = f64(np.asarray(w, np.float32).astype(ml_dtypes.bfloat16)).reshape(k // 32, 32, n)
    amax = np.abs(w).max(1)
    byte = np.clip(np.where(amax > 0, np.frexp(amax)[1] - 1 + 127 - 7, 1), 1, 254)
    scaled = (w * np.exp2(127.0 - byte)[:, None, :]).reshape(k, n).astype(np.float32)
    words = np.ascontiguousarray(scaled.reshape(k // 512, 128, 4, n).transpose(0, 1, 3, 2)).astype(ml_dtypes.float8_e4m3fn).view(np.uint8)
    return words, np.ascontiguousarray(byte.astype(np.uint8).reshape(k // 512, 16, n))


def unpack_weight(words, scales):
    g, p, n, _ = words.shape
    vals = np.ascontiguousarray(words).view(ml_dtypes.float8_e4m3fn).astype(np.float64) * np.repeat(np.exp2(scales.astype(np.float64) - 127.0), 8, axis=1)[..., None]
    return vals.transpose(0, 1, 3, 2).reshape(g * 512, n)


def sigmoid(v):
    return 1.0 / (1.0 + np.exp(-np.maximum(v, -700.0)))


K, T, S, H, G = 512, 2048, 512, 512, 2048
P = 2 ** 7


def setup_inputs():
    n = np.random.standard_normal
    s = mx_kscale(K)[:, None]
    packed_xT = pack_weight(n((K, T)) * s)
    packed_dT = pack_weight(n((K, G)) / s)
    return {
        "x_words": packed_xT[0],
        "x_scales": packed_xT[1],
        "w1": (n((K, H)) / np.sqrt(K) / s).astype(np.float32),
        "cr": np.tile(np.random.uniform(0.0, 1.0, S), (P, 1)).astype(np.float32),
        "gs": (np.random.uniform(0.5, 1.5, (K, 1)) * s).astype(np.float32),
        "d_words": packed_dT[0],
        "d_scales": packed_dT[1],
        "offs": striped(np.random.permutation(T)[:S]),
        "r1": striped8(np.stack([np.random.permutation(S) for _ in range(8)])),
        "r2": striped8(np.stack([np.random.permutation(S) for _ in range(8)])),
        "r3": striped8(np.stack([np.random.permutation(S) for _ in range(8)])),
        "kq": striped8(np.random.randint(0, G, (8, H))),
    }


def reference(x_words, x_scales, w1, cr, gs, d_words, d_scales, offs, r1, r2, r3, kq):
    d_kq = unpack_weight(d_words, d_scales)[np.arange(K)[:, None], runs(kq, K)]
    xq = unpack_weight(x_words, x_scales)[:, unstriped(offs)]
    y = mxq(f64(w1), 0, "e4m3").T @ xq
    v1 = y[np.arange(H)[:, None], runs(r1, H)] + 0.5 * (y[np.arange(H)[:, None], runs(r2, H)] - (y[np.arange(H)[:, None], runs(r3, H)]))
    tr = y + f64(cr)[:1] * (v1 - y)
    z = f64(gs) * (tr * sigmoid(tr - y))
    return 0.0625 * ((d_kq.T @ mxq(z, 0, "e4m3")))

@@ -1,0 +1,217 @@
+from contextlib import ExitStack
+
+import concourse.mybir as mybir
+from concourse.masks import make_identity
+
+K, T, S, H, G = 512, 2048, 512, 512, 2048
+FLOPS = 2 * K * H * S + 2 * H * H * S
+
+F32 = mybir.dt.float32
+BF16 = mybir.dt.bfloat16
+I32 = mybir.dt.int32
+U32 = mybir.dt.uint32
+U16 = mybir.dt.uint16
+U8 = mybir.dt.uint8
+FP8X4 = mybir.dt.float8_e4m3fn_x4
+ACT = mybir.ActivationFunctionType
+ALU = mybir.AluOpType
+
+P = 128
+PACK = 4
+BLOCK = 128
+LINE = 4
+GATHER_BUFS = 6
+W_PIECES = ((0, 192), (192, 384), (384, 512))
+
+
+def tile_picked_diffevo_none_p_kernel(
+    tc, x_words, x_scales, w1, cr, gs, d_words, d_scales, offs, r1, r2, r3, kq, out
+):
+    nc = tc.nc
+    with ExitStack() as ctx:
+        keep = ctx.enter_context(tc.tile_pool(name="keep", bufs=1))
+        ring = ctx.enter_context(tc.tile_pool(name="ring", bufs=2))
+        psum = ctx.enter_context(tc.psum_pool(name="psum", bufs=8))
+
+        def load_list(src, name):
+            tile = keep.tile([P, S // 16], U16, name=name)
+            nc.sync.dma_start(tile[:], src)
+            return tile
+
+        x_scale_table = keep.tile([P, T], U8, align_bytes=64)
+        nc.vector.memset(x_scale_table[:].bitcast(I32), 0)
+        warm = keep.tile([P, 8], F32)
+        nc.gpsimd.memset(warm[:], 0.0)
+        nc.scalar.activation(warm[:, 0:1], warm[:, 1:2], ACT.Sigmoid)
+        d_scale_table = keep.tile([P, G], U8, align_bytes=64)
+        nc.gpsimd.memset(d_scale_table[:].bitcast(I32), 0)
+        d_scale_plane = keep.tile([P, H], U8, align_bytes=64)
+        nc.gpsimd.memset(d_scale_plane[:].bitcast(I32), 0)
+        ident = keep.tile([P, P], F32)
+        make_identity(nc, ident[:])
+
+        offs_sb = load_list(offs, "offs_sb")
+        x_scale_rows = x_scales[0].rearrange("(q r) n -> r q n", r=4)
+        for r in range(4):
+            nc.sync.dma_start(x_scale_table[r:P:32, :].bitcast(I32), x_scale_rows[r].bitcast(I32))
+        x_table = keep.tile([P, T], U32, align_bytes=64)
+        nc.sync.dma_start(x_table[:].bitcast(I32), x_words[0].rearrange("p n t -> p (n t)").bitcast(I32))
+        w_rows = w1.rearrange("(p j) c -> p j c", j=PACK)
+        w_pieces = []
+        for u, (c0, c1) in enumerate(W_PIECES):
+            piece = keep.tile([P, PACK, c1 - c0], F32, name="w_piece%d" % u)
+            nc.sync.dma_start(piece[:], w_rows[:, :, c0:c1])
+            w_pieces.append(piece)
+        kq_sb = load_list(kq, "kq_sb")
+        nc.sync.dma_start(d_scale_table[0:P:8, :].bitcast(I32), d_scales[0].bitcast(I32))
+        lists = [load_list(r1, "r1_sb"), load_list(r2, "r2_sb"), load_list(r3, "r3_sb")]
+        gs_sb = keep.tile([P, PACK], F32)
+        nc.sync.dma_start(gs_sb[:], gs.rearrange("(p t) o -> p (t o)", t=PACK))
+        cr_sb = keep.tile([P, S // BLOCK], F32)
+        with nc.allow_non_contiguous_dma(reason="one value of cr for each partition and block"):
+            nc.sync.dma_start(cr_sb[:], cr[0].rearrange("(b p) -> p b", p=P))
+        d_table = keep.tile([P, G], U32, align_bytes=64)
+        nc.sync.dma_start(d_table[:].bitcast(I32), d_words[0].rearrange("p n t -> p (n t)").bitcast(I32))
+
+        x_plane = keep.tile([P, S], U8, align_bytes=64)
+        nc.vector.tensor_copy(x_plane[:], x_scale_table[:].indirect(offs_sb[:]))
+        x_codes = keep.tile([P, S], U32, align_bytes=64)
+        nc.vector.tensor_copy(x_codes[:], x_table[:].indirect(offs_sb[:]))
+
+        w_bf = keep.tile([P, PACK, P, PACK], BF16, align_bytes=64)
+        for (c0, c1), piece, engine_copy in zip(W_PIECES, w_pieces, (nc.scalar.copy, nc.vector.tensor_copy, nc.vector.tensor_copy)):
+            engine_copy(
+                w_bf[:, :, c0 // PACK : c1 // PACK, :].rearrange("p t m j -> p m j t"),
+                piece[:].rearrange("p j (m t) -> p m j t", t=PACK),
+            )
+        w_codes = keep.tile([P, PACK, P], U32, align_bytes=64)
+        w_plane = keep.tile([P, PACK, P], U8, align_bytes=64)
+        y_banks = []
+        neg_y = []
+        for t in range(PACK):
+            nc.vector.quantize_mx(
+                out=w_codes[:, t, :].bitcast(FP8X4),
+                scales=w_plane[:, t, :],
+                in_=w_bf[:, t, :, :].rearrange("p m j -> p (m j)"),
+            )
+            bank = psum.tile([P, S], F32, name="y_bank", tag="bank")
+            nc.tensor.matmul_mx(
+                out=bank[:],
+                lhsT=w_codes[:, t, :].bitcast(FP8X4),
+                lhsT_scale=w_plane[:, t, :],
+                rhs=x_codes[:].bitcast(FP8X4),
+                rhs_scale=x_plane[:],
+                start=True,
+                stop=True,
+            )
+            window = keep.tile([P, S], F32, name="neg_y%d" % t, tag="neg_y%d" % t)
+            nc.scalar.activation(window[:], bank[:], ACT.Copy, scale=-1.0)
+            y_banks.append(bank)
+            neg_y.append(window)
+        gs_y = keep.tile([P, PACK, S], F32)
+        for t in range(PACK):
+            nc.scalar.activation(gs_y[:, t, :], y_banks[t][:], ACT.Copy, scale=gs_sb[:, t : t + 1])
+
+        d_picked_scales = keep.tile([P, H], U8, align_bytes=64)
+        nc.vector.tensor_copy(d_picked_scales[:], d_scale_table[:].indirect(kq_sb[:]))
+        for r in range(4):
+            nc.sync.dma_start(
+                d_scale_plane[r:P:32, :].bitcast(I32), d_picked_scales[8 * r : P : 32, :].bitcast(I32)
+            )
+        d_codes = keep.tile([P, H], U32, align_bytes=64)
+
+        factors = (-1.0, -0.5, 0.5)
+        out_view = out.rearrange("(m p) j -> p m j", p=P)
+
+        def look_up(start, width, part):
+            blocks = width // BLOCK
+            entries = slice(start // 16, (start + width) // 16)
+            step_t = psum.tile([P, blocks, len(part), P], F32, name="step_t", tag="bank")
+            for at, t in enumerate(part):
+                picked = []
+                for n in range(3):
+                    tile = ring.tile([P, width], F32, name="picked", bufs=GATHER_BUFS)
+                    nc.vector.tensor_scalar(
+                        tile[:], neg_y[t][:].indirect(lists[n][:, entries]), factors[n], 0.0, ALU.mult, ALU.add
+                    )
+                    picked.append(tile)
+                for b in range(blocks):
+                    first = start + b * BLOCK
+                    terms = [neg_y[t][:, first : first + BLOCK]]
+                    terms.extend(tile[:, b * BLOCK : (b + 1) * BLOCK] for tile in picked)
+                    for n, term in enumerate(terms):
+                        nc.tensor.matmul(
+                            step_t[:, b, at, :], term, ident[:], start=(n == 0), stop=(n == 3), is_transpose=True
+                        )
+            gain_t = ring.tile([P, blocks, len(part), P], F32, name="gain_t")
+            gain = psum.tile([P, len(part), width], F32, name="gain", tag="bank")
+            for b in range(blocks):
+                column = start // BLOCK + b
+                nc.scalar.activation(gain_t[:, b], step_t[:, b], ACT.Copy, scale=cr_sb[:, column : column + 1])
+                for at in range(len(part)):
+                    nc.tensor.transpose(gain[:, at, b * BLOCK : (b + 1) * BLOCK], gain_t[:, b, at, :], ident[:])
+            return gain
+
+        def finish(start, width, parts, gains, trial, last):
+            cols = slice(start, start + width)
+            sig = ring.tile([P, width // LINE, PACK, LINE], F32, name="sig")
+            for part, gain in zip(parts, gains):
+                nc.scalar.activation(
+                    sig[:, :, part[0] : part[-1] + 1, :], gain[:].rearrange("p t (c i) -> p c t i", i=LINE), ACT.Sigmoid
+                )
+                for at, t in enumerate(part):
+                    nc.vector.scalar_tensor_tensor(
+                        trial[:, :, t, :],
+                        gain[:, at, :].rearrange("p (c i) -> p c i", i=LINE),
+                        gs_sb[:, t : t + 1],
+                        gs_y[:, t, cols].rearrange("p (c i) -> p c i", i=LINE),
+                        ALU.mult,
+                        ALU.add,
+                    )
+            z_bf = ring.tile([P, width // LINE, LINE, PACK], BF16, name="z_bf", align_bytes=64)
+            nc.vector.tensor_tensor(z_bf[:].rearrange("p c i t -> p c t i"), trial[:], sig[:], ALU.mult)
+            z_codes = ring.tile([P, width], U32, name="z_codes", align_bytes=64)
+            z_plane = ring.tile([P, width], U8, name="z_plane", align_bytes=64)
+            nc.vector.quantize_mx(
+                out=z_codes[:].bitcast(FP8X4), scales=z_plane[:], in_=z_bf[:].rearrange("p c i t -> p (c i t)")
+            )
+            per_bank = 2 if last else S // width
+            for m0 in range(0, H // P, per_bank):
+                acc = psum.tile([P, per_bank, width], F32, name="acc", tag="bank")
+                for m in range(per_bank):
+                    rows = slice((m0 + m) * P, (m0 + m + 1) * P)
+                    nc.tensor.matmul_mx(
+                        out=acc[:, m, :],
+                        lhsT=d_codes[:, rows].bitcast(FP8X4),
+                        lhsT_scale=d_scale_plane[:, rows],
+                        rhs=z_codes[:].bitcast(FP8X4),
+                        rhs_scale=z_plane[:],
+                        start=True,
+                        stop=True,
+                    )
+                result = ring.tile([P, per_bank, width], F32, name="result", bufs=5)
+                if last and m0 == 0:
+                    nc.vector.tensor_scalar(result[:], acc[:], 0.0625, None, ALU.mult)
+                    nc.sync.dma_start(out_view[:, m0 : m0 + per_bank, cols], result[:])
+                else:
+                    nc.scalar.activation(result[:], acc[:], ACT.Copy, scale=0.0625)
+                    queue = nc.scalar if last else nc.sync
+                    queue.dma_start(out_view[:, m0 : m0 + per_bank, cols], result[:])
+
+        wide = (0, 256, ((0, 1), (2, 3)))
+        middle = (256, 128, ((0, 1, 2, 3),))
+        final = (384, 128, ((0, 1, 2), (3,)))
+
+        def look_up_chunk(chunk):
+            return [look_up(chunk[0], chunk[1], part) for part in chunk[2]]
+
+        def trial_tile(chunk, tag):
+            return keep.tile([P, chunk[1] // LINE, PACK, LINE], F32, name="trial", tag=tag)
+
+        wide_gains = look_up_chunk(wide)
+        nc.vector.tensor_copy(d_codes[:], d_table[:].indirect(kq_sb[:]))
+        middle_gains = look_up_chunk(middle)
+        finish(*wide, wide_gains, trial_tile(wide, "trial_wide"), False)
+        final_gains = look_up_chunk(final)
+        finish(*middle, middle_gains, trial_tile(middle, "neg_y3"), False)
+        finish(*final, final_gains, trial_tile(final, "trial_final"), True)

@@ -20,8 +20,8 @@ P = 128
 PACK = 4
 BLOCK = 128
 LINE = 4
-GATHER_BUFS = 6
-W_PIECES = ((0, 192), (192, 384), (384, 512))
+GATHER_BUFS = 27
+W_PIECES = ((0, 192), (192, 320), (320, 512))
 
 
 def tile_picked_diffevo_none_p_kernel(
@@ -31,39 +31,39 @@ def tile_picked_diffevo_none_p_kernel(
     with ExitStack() as ctx:
         keep = ctx.enter_context(tc.tile_pool(name="keep", bufs=1))
         ring = ctx.enter_context(tc.tile_pool(name="ring", bufs=2))
-        psum = ctx.enter_context(tc.psum_pool(name="psum", bufs=8))
+        psum = ctx.enter_context(tc.psum_pool(name="psum", bufs=1))
 
         def load_list(src, name):
             tile = keep.tile([P, S // 16], U16, name=name)
             nc.sync.dma_start(tile[:], src)
             return tile
 
+        d_scale_table = keep.tile([P, G], U8, align_bytes=64)
+        nc.gpsimd.memset(d_scale_table[:].bitcast(I32), 0)
         x_scale_table = keep.tile([P, T], U8, align_bytes=64)
         nc.vector.memset(x_scale_table[:].bitcast(I32), 0)
         warm = keep.tile([P, 8], F32)
-        nc.gpsimd.memset(warm[:], 0.0)
+        nc.vector.memset(warm[:], 0.0)
         nc.scalar.activation(warm[:, 0:1], warm[:, 1:2], ACT.Sigmoid)
-        d_scale_table = keep.tile([P, G], U8, align_bytes=64)
-        nc.gpsimd.memset(d_scale_table[:].bitcast(I32), 0)
         d_scale_plane = keep.tile([P, H], U8, align_bytes=64)
         nc.gpsimd.memset(d_scale_plane[:].bitcast(I32), 0)
         ident = keep.tile([P, P], F32)
         make_identity(nc, ident[:])
 
+        kq_sb = load_list(kq, "kq_sb")
+        nc.sync.dma_start(d_scale_table[0:P:8, :].bitcast(I32), d_scales[0].bitcast(I32))
         offs_sb = load_list(offs, "offs_sb")
+        x_table = keep.tile([P, T], U32, align_bytes=64)
+        nc.sync.dma_start(x_table[:].bitcast(I32), x_words[0].rearrange("p n t -> p (n t)").bitcast(I32))
         x_scale_rows = x_scales[0].rearrange("(q r) n -> r q n", r=4)
         for r in range(4):
             nc.sync.dma_start(x_scale_table[r:P:32, :].bitcast(I32), x_scale_rows[r].bitcast(I32))
-        x_table = keep.tile([P, T], U32, align_bytes=64)
-        nc.sync.dma_start(x_table[:].bitcast(I32), x_words[0].rearrange("p n t -> p (n t)").bitcast(I32))
         w_rows = w1.rearrange("(p j) c -> p j c", j=PACK)
         w_pieces = []
         for u, (c0, c1) in enumerate(W_PIECES):
             piece = keep.tile([P, PACK, c1 - c0], F32, name="w_piece%d" % u)
             nc.sync.dma_start(piece[:], w_rows[:, :, c0:c1])
             w_pieces.append(piece)
-        kq_sb = load_list(kq, "kq_sb")
-        nc.sync.dma_start(d_scale_table[0:P:8, :].bitcast(I32), d_scales[0].bitcast(I32))
         lists = [load_list(r1, "r1_sb"), load_list(r2, "r2_sb"), load_list(r3, "r3_sb")]
         gs_sb = keep.tile([P, PACK], F32)
         nc.sync.dma_start(gs_sb[:], gs.rearrange("(p t) o -> p (t o)", t=PACK))
@@ -73,13 +73,15 @@ def tile_picked_diffevo_none_p_kernel(
         d_table = keep.tile([P, G], U32, align_bytes=64)
         nc.sync.dma_start(d_table[:].bitcast(I32), d_words[0].rearrange("p n t -> p (n t)").bitcast(I32))
 
-        x_plane = keep.tile([P, S], U8, align_bytes=64)
-        nc.vector.tensor_copy(x_plane[:], x_scale_table[:].indirect(offs_sb[:]))
+        d_picked_scales = keep.tile([P, H], U8, align_bytes=64)
+        nc.vector.tensor_copy(d_picked_scales[:], d_scale_table[:].indirect(kq_sb[:]))
         x_codes = keep.tile([P, S], U32, align_bytes=64)
         nc.vector.tensor_copy(x_codes[:], x_table[:].indirect(offs_sb[:]))
+        x_plane = keep.tile([P, S], U8, align_bytes=64)
+        nc.vector.tensor_copy(x_plane[:], x_scale_table[:].indirect(offs_sb[:]))
 
         w_bf = keep.tile([P, PACK, P, PACK], BF16, align_bytes=64)
-        for (c0, c1), piece, engine_copy in zip(W_PIECES, w_pieces, (nc.scalar.copy, nc.vector.tensor_copy, nc.vector.tensor_copy)):
+        for (c0, c1), piece, engine_copy in zip(W_PIECES, w_pieces, (nc.scalar.copy, nc.scalar.copy, nc.vector.tensor_copy)):
             engine_copy(
                 w_bf[:, :, c0 // PACK : c1 // PACK, :].rearrange("p t m j -> p m j t"),
                 piece[:].rearrange("p j (m t) -> p m j t", t=PACK),
@@ -94,26 +96,29 @@ def tile_picked_diffevo_none_p_kernel(
                 scales=w_plane[:, t, :],
                 in_=w_bf[:, t, :, :].rearrange("p m j -> p (m j)"),
             )
-            bank = psum.tile([P, S], F32, name="y_bank", tag="bank")
-            nc.tensor.matmul_mx(
-                out=bank[:],
-                lhsT=w_codes[:, t, :].bitcast(FP8X4),
-                lhsT_scale=w_plane[:, t, :],
-                rhs=x_codes[:].bitcast(FP8X4),
-                rhs_scale=x_plane[:],
-                start=True,
-                stop=True,
-            )
-            window = keep.tile([P, S], F32, name="neg_y%d" % t, tag="neg_y%d" % t)
-            nc.scalar.activation(window[:], bank[:], ACT.Copy, scale=-1.0)
-            y_banks.append(bank)
+            window = keep.tile([P, S], F32, name="neg_y%d" % t)
             neg_y.append(window)
+            spans = ((0, S // 2), (S // 2, S)) if t == 0 else ((0, S),)
+            for c0, c1 in spans:
+                bank = psum.tile([P, c1 - c0], F32, name="y_bank", tag="bank%d" % len(y_banks))
+                nc.tensor.matmul_mx(
+                    out=bank[:],
+                    lhsT=w_codes[:, t, :].bitcast(FP8X4),
+                    lhsT_scale=w_plane[:, t, :],
+                    rhs=x_codes[:, c0:c1].bitcast(FP8X4),
+                    rhs_scale=x_plane[:, c0:c1],
+                    start=True,
+                    stop=True,
+                )
+                if t == 0 and c0 > 0:
+                    nc.vector.tensor_scalar(window[:, c0:c1], bank[:], -1.0, None, ALU.mult)
+                else:
+                    nc.scalar.activation(window[:, c0:c1], bank[:], ACT.Copy, scale=-1.0)
+                y_banks.append((t, c0, c1, bank))
         gs_y = keep.tile([P, PACK, S], F32)
-        for t in range(PACK):
-            nc.scalar.activation(gs_y[:, t, :], y_banks[t][:], ACT.Copy, scale=gs_sb[:, t : t + 1])
+        for t, c0, c1, bank in y_banks:
+            nc.scalar.activation(gs_y[:, t, c0:c1], bank[:], ACT.Copy, scale=gs_sb[:, t : t + 1])
 
-        d_picked_scales = keep.tile([P, H], U8, align_bytes=64)
-        nc.vector.tensor_copy(d_picked_scales[:], d_scale_table[:].indirect(kq_sb[:]))
         for r in range(4):
             nc.sync.dma_start(
                 d_scale_plane[r:P:32, :].bitcast(I32), d_picked_scales[8 * r : P : 32, :].bitcast(I32)
@@ -123,10 +128,10 @@ def tile_picked_diffevo_none_p_kernel(
         factors = (-1.0, -0.5, 0.5)
         out_view = out.rearrange("(m p) j -> p m j", p=P)
 
-        def look_up(start, width, part):
+        def look_up(start, width, part, step_bank, gain_bank):
             blocks = width // BLOCK
             entries = slice(start // 16, (start + width) // 16)
-            step_t = psum.tile([P, blocks, len(part), P], F32, name="step_t", tag="bank")
+            step_t = psum.tile([P, blocks, len(part), P], F32, name="step_t", tag="bank%d" % step_bank)
             for at, t in enumerate(part):
                 picked = []
                 for n in range(3):
@@ -143,8 +148,8 @@ def tile_picked_diffevo_none_p_kernel(
                         nc.tensor.matmul(
                             step_t[:, b, at, :], term, ident[:], start=(n == 0), stop=(n == 3), is_transpose=True
                         )
-            gain_t = ring.tile([P, blocks, len(part), P], F32, name="gain_t")
-            gain = psum.tile([P, len(part), width], F32, name="gain", tag="bank")
+            gain_t = ring.tile([P, blocks, len(part), P], F32, name="gain_t", bufs=3)
+            gain = psum.tile([P, len(part), width], F32, name="gain", tag="bank%d" % gain_bank)
             for b in range(blocks):
                 column = start // BLOCK + b
                 nc.scalar.activation(gain_t[:, b], step_t[:, b], ACT.Copy, scale=cr_sb[:, column : column + 1])
@@ -152,32 +157,44 @@ def tile_picked_diffevo_none_p_kernel(
                     nc.tensor.transpose(gain[:, at, b * BLOCK : (b + 1) * BLOCK], gain_t[:, b, at, :], ident[:])
             return gain
 
-        def finish(start, width, parts, gains, trial, last):
-            cols = slice(start, start + width)
-            sig = ring.tile([P, width // LINE, PACK, LINE], F32, name="sig")
-            for part, gain in zip(parts, gains):
-                nc.scalar.activation(
-                    sig[:, :, part[0] : part[-1] + 1, :], gain[:].rearrange("p t (c i) -> p c t i", i=LINE), ACT.Sigmoid
+        sig = keep.tile([P, S // LINE, PACK, LINE], F32)
+
+        def blend(start, width, part, gain, trial, trial_start):
+            groups = slice(start // LINE, (start + width) // LINE)
+            nc.scalar.activation(
+                sig[:, groups, part[0] : part[-1] + 1, :], gain[:].rearrange("p t (c i) -> p c t i", i=LINE), ACT.Sigmoid
+            )
+            for at, t in enumerate(part):
+                nc.vector.scalar_tensor_tensor(
+                    trial[:, groups, t, :],
+                    gain[:, at, :].rearrange("p (c i) -> p c i", i=LINE),
+                    gs_sb[:, t : t + 1],
+                    gs_y[:, t, start : start + width].rearrange("p (c i) -> p c i", i=LINE),
+                    ALU.mult,
+                    ALU.add,
                 )
-                for at, t in enumerate(part):
-                    nc.vector.scalar_tensor_tensor(
-                        trial[:, :, t, :],
-                        gain[:, at, :].rearrange("p (c i) -> p c i", i=LINE),
-                        gs_sb[:, t : t + 1],
-                        gs_y[:, t, cols].rearrange("p (c i) -> p c i", i=LINE),
-                        ALU.mult,
-                        ALU.add,
-                    )
-            z_bf = ring.tile([P, width // LINE, LINE, PACK], BF16, name="z_bf", align_bytes=64)
-            nc.vector.tensor_tensor(z_bf[:].rearrange("p c i t -> p c t i"), trial[:], sig[:], ALU.mult)
-            z_codes = ring.tile([P, width], U32, name="z_codes", align_bytes=64)
-            z_plane = ring.tile([P, width], U8, name="z_plane", align_bytes=64)
+
+        def weigh(start, width, trial, trial_start):
+            groups = slice(start // LINE, (start + width) // LINE)
+            z_bf = ring.tile([P, width // LINE, LINE, PACK], BF16, name="z_bf", align_bytes=64, bufs=3)
+            nc.vector.tensor_tensor(
+                z_bf[:].rearrange("p c i t -> p c t i"),
+                trial[:, groups],
+                sig[:, groups],
+                ALU.mult,
+            )
+            return z_bf
+
+        def finish(start, width, z_bf, banks, last):
+            cols = slice(start, start + width)
+            z_codes = ring.tile([P, width], U32, name="z_codes", align_bytes=64, bufs=3)
+            z_plane = ring.tile([P, width], U8, name="z_plane", align_bytes=64, bufs=3)
             nc.vector.quantize_mx(
                 out=z_codes[:].bitcast(FP8X4), scales=z_plane[:], in_=z_bf[:].rearrange("p c i t -> p (c i t)")
             )
             per_bank = 2 if last else S // width
             for m0 in range(0, H // P, per_bank):
-                acc = psum.tile([P, per_bank, width], F32, name="acc", tag="bank")
+                acc = psum.tile([P, per_bank, width], F32, name="acc", tag="bank%d" % banks[m0 // per_bank])
                 for m in range(per_bank):
                     rows = slice((m0 + m) * P, (m0 + m + 1) * P)
                     nc.tensor.matmul_mx(
@@ -198,20 +215,29 @@ def tile_picked_diffevo_none_p_kernel(
                     queue = nc.scalar if last else nc.sync
                     queue.dma_start(out_view[:, m0 : m0 + per_bank, cols], result[:])
 
-        wide = (0, 256, ((0, 1), (2, 3)))
-        middle = (256, 128, ((0, 1, 2, 3),))
-        final = (384, 128, ((0, 1, 2), (3,)))
-
-        def look_up_chunk(chunk):
-            return [look_up(chunk[0], chunk[1], part) for part in chunk[2]]
-
-        def trial_tile(chunk, tag):
-            return keep.tile([P, chunk[1] // LINE, PACK, LINE], F32, name="trial", tag=tag)
-
-        wide_gains = look_up_chunk(wide)
+        half = S // 2
+        first_trial = keep.tile([P, S // LINE, PACK, LINE], F32)
+        second_trial = first_trial
+        steps = [
+            (0, half, (0, 1)),
+            (0, half, (2, 3)),
+            (half, half, (0, 1)),
+            (half, half, (2,)),
+            (half, BLOCK, (3,)),
+            (half + BLOCK, BLOCK, (3,)),
+        ]
+        banks = [(5, 6), (7, 0), (1, 2), (3, 4), (5, 7), (1, 3)]
+        gains = [look_up(*step, *pair) for step, pair in zip(steps, banks)]
         nc.vector.tensor_copy(d_codes[:], d_table[:].indirect(kq_sb[:]))
-        middle_gains = look_up_chunk(middle)
-        finish(*wide, wide_gains, trial_tile(wide, "trial_wide"), False)
-        final_gains = look_up_chunk(final)
-        finish(*middle, middle_gains, trial_tile(middle, "neg_y3"), False)
-        finish(*final, final_gains, trial_tile(final, "trial_final"), True)
+        for n in range(2):
+            blend(*steps[n], gains[n], first_trial, 0)
+        blend(*steps[2], gains[2], second_trial, half)
+        z_first = weigh(0, half, first_trial, 0)
+        blend(*steps[3], gains[3], second_trial, half)
+        blend(*steps[4], gains[4], second_trial, half)
+        finish(0, half, z_first, (1, 5), False)
+        z_third = weigh(half, BLOCK, second_trial, half)
+        blend(*steps[5], gains[5], second_trial, half)
+        finish(half, BLOCK, z_third, (6,), False)
+        z_fourth = weigh(half + BLOCK, BLOCK, second_trial, half)
+        finish(half + BLOCK, BLOCK, z_fourth, (0, 2), True)

@@ -21,7 +21,7 @@ PACK = 4
 BLOCK = 128
 LINE = 4
 GATHER_BUFS = 27
-W_PIECES = ((0, 192), (192, 320), (320, 512))
+W_SPLIT = 176
 
 
 def tile_picked_diffevo_none_p_kernel(
@@ -50,23 +50,21 @@ def tile_picked_diffevo_none_p_kernel(
         ident = keep.tile([P, P], F32)
         make_identity(nc, ident[:])
 
+        offs_sb = load_list(offs, "offs_sb")
         kq_sb = load_list(kq, "kq_sb")
         nc.sync.dma_start(d_scale_table[0:P:8, :].bitcast(I32), d_scales[0].bitcast(I32))
-        offs_sb = load_list(offs, "offs_sb")
-        x_table = keep.tile([P, T], U32, align_bytes=64)
-        nc.sync.dma_start(x_table[:].bitcast(I32), x_words[0].rearrange("p n t -> p (n t)").bitcast(I32))
         x_scale_rows = x_scales[0].rearrange("(q r) n -> r q n", r=4)
         for r in range(4):
             nc.sync.dma_start(x_scale_table[r:P:32, :].bitcast(I32), x_scale_rows[r].bitcast(I32))
-        w_rows = w1.rearrange("(p j) c -> p j c", j=PACK)
-        w_pieces = []
-        for u, (c0, c1) in enumerate(W_PIECES):
-            piece = keep.tile([P, PACK, c1 - c0], F32, name="w_piece%d" % u)
-            nc.sync.dma_start(piece[:], w_rows[:, :, c0:c1])
-            w_pieces.append(piece)
-        lists = [load_list(r1, "r1_sb"), load_list(r2, "r2_sb"), load_list(r3, "r3_sb")]
+        w_raw = keep.tile([P, PACK, H], F32)
+        nc.sync.dma_start(w_raw[:], w1.rearrange("(p j) c -> p j c", j=PACK))
+        x_table = keep.tile([P, T], U32, align_bytes=64)
+        nc.sync.dma_start(x_table[:].bitcast(I32), x_words[0].rearrange("p n t -> p (n t)").bitcast(I32))
         gs_sb = keep.tile([P, PACK], F32)
         nc.sync.dma_start(gs_sb[:], gs.rearrange("(p t) o -> p (t o)", t=PACK))
+        r3_sb = load_list(r3, "r3_sb")
+        r2_sb = load_list(r2, "r2_sb")
+        r1_sb = load_list(r1, "r1_sb")
         cr_sb = keep.tile([P, S // BLOCK], F32)
         with nc.allow_non_contiguous_dma(reason="one value of cr for each partition and block"):
             nc.sync.dma_start(cr_sb[:], cr[0].rearrange("(b p) -> p b", p=P))
@@ -75,32 +73,44 @@ def tile_picked_diffevo_none_p_kernel(
 
         d_picked_scales = keep.tile([P, H], U8, align_bytes=64)
         nc.vector.tensor_copy(d_picked_scales[:], d_scale_table[:].indirect(kq_sb[:]))
-        x_codes = keep.tile([P, S], U32, align_bytes=64)
-        nc.vector.tensor_copy(x_codes[:], x_table[:].indirect(offs_sb[:]))
         x_plane = keep.tile([P, S], U8, align_bytes=64)
         nc.vector.tensor_copy(x_plane[:], x_scale_table[:].indirect(offs_sb[:]))
 
         w_bf = keep.tile([P, PACK, P, PACK], BF16, align_bytes=64)
-        for (c0, c1), piece, engine_copy in zip(W_PIECES, w_pieces, (nc.scalar.copy, nc.scalar.copy, nc.vector.tensor_copy)):
+        for c0, c1, engine_copy in ((0, W_SPLIT, nc.scalar.copy), (W_SPLIT, H, nc.vector.tensor_copy)):
             engine_copy(
                 w_bf[:, :, c0 // PACK : c1 // PACK, :].rearrange("p t m j -> p m j t"),
-                piece[:].rearrange("p j (m t) -> p m j t", t=PACK),
+                w_raw[:, :, c0:c1].rearrange("p j (m t) -> p m j t", t=PACK),
             )
         w_codes = keep.tile([P, PACK, P], U32, align_bytes=64)
         w_plane = keep.tile([P, PACK, P], U8, align_bytes=64)
-        y_banks = []
-        neg_y = []
         for t in range(PACK):
             nc.vector.quantize_mx(
                 out=w_codes[:, t, :].bitcast(FP8X4),
                 scales=w_plane[:, t, :],
                 in_=w_bf[:, t, :, :].rearrange("p m j -> p (m j)"),
             )
-            window = keep.tile([P, S], F32, name="neg_y%d" % t)
-            neg_y.append(window)
-            spans = ((0, S // 2), (S // 2, S)) if t == 0 else ((0, S),)
-            for c0, c1 in spans:
-                bank = psum.tile([P, c1 - c0], F32, name="y_bank", tag="bank%d" % len(y_banks))
+
+        half = S // 2
+        x_codes = keep.tile([P, S], U32, align_bytes=64)
+        nc.vector.tensor_copy(x_codes[:, :half], x_table[:].indirect(offs_sb[:, : half // 16]))
+        half_gs = keep.tile([P, PACK], F32)
+        nc.vector.tensor_scalar(half_gs[:], gs_sb[:], 0.5, None, ALU.mult)
+        nc.vector.tensor_copy(x_codes[:, half:], x_table[:].indirect(offs_sb[:, half // 16 :]))
+        safe_gs = keep.tile([P, PACK], F32)
+        nc.vector.scalar_tensor_tensor(safe_gs[:], gs_sb[:], 0.0, gs_sb[:], ALU.is_equal, ALU.add)
+        inv_gs = keep.tile([P, PACK], F32)
+        nc.vector.reciprocal(inv_gs[:], safe_gs[:])
+
+        y_full = []
+        y_half = []
+        y_spans = [(0, 0, half, 4), (0, half, S, 5), (1, 0, S, 0), (2, 0, S, 1), (3, 0, S, 2)]
+        for t in range(PACK):
+            y_full.append(keep.tile([P, S], F32, name="y_full%d" % t))
+            y_half.append(keep.tile([P, S], F32, name="y_half%d" % t))
+            made = []
+            for c0, c1, bank_number in [span[1:] for span in y_spans if span[0] == t]:
+                bank = psum.tile([P, c1 - c0], F32, name="y_bank", tag="bank%d" % bank_number)
                 nc.tensor.matmul_mx(
                     out=bank[:],
                     lhsT=w_codes[:, t, :].bitcast(FP8X4),
@@ -110,93 +120,123 @@ def tile_picked_diffevo_none_p_kernel(
                     start=True,
                     stop=True,
                 )
-                if t == 0 and c0 > 0:
-                    nc.vector.tensor_scalar(window[:, c0:c1], bank[:], -1.0, None, ALU.mult)
+                if c0 > 0:
+                    nc.vector.tensor_scalar(y_half[t][:, c0:c1], bank[:], half_gs[:, t : t + 1], None, ALU.mult)
                 else:
-                    nc.scalar.activation(window[:, c0:c1], bank[:], ACT.Copy, scale=-1.0)
-                y_banks.append((t, c0, c1, bank))
-        gs_y = keep.tile([P, PACK, S], F32)
-        for t, c0, c1, bank in y_banks:
-            nc.scalar.activation(gs_y[:, t, c0:c1], bank[:], ACT.Copy, scale=gs_sb[:, t : t + 1])
+                    nc.scalar.activation(y_half[t][:, c0:c1], bank[:], ACT.Copy, scale=half_gs[:, t : t + 1])
+                made.append((c0, c1, bank))
+            for c0, c1, bank in made:
+                nc.scalar.activation(y_full[t][:, c0:c1], bank[:], ACT.Copy, scale=gs_sb[:, t : t + 1])
 
         for r in range(4):
             nc.sync.dma_start(
                 d_scale_plane[r:P:32, :].bitcast(I32), d_picked_scales[8 * r : P : 32, :].bitcast(I32)
             )
-        d_codes = keep.tile([P, H], U32, align_bytes=64)
 
-        factors = (-1.0, -0.5, 0.5)
-        out_view = out.rearrange("(m p) j -> p m j", p=P)
+        y_turned = keep.tile([P, PACK, S // BLOCK, P], F32)
+        taken = []
 
-        def look_up(start, width, part, step_bank, gain_bank):
-            blocks = width // BLOCK
+        def passing_bank(shape):
+            bank = psum.tile(shape, F32, name="passing", tag="bank%d" % (4 + (len(taken) + 2) % 4))
+            taken.append(bank)
+            return bank
+
+        def turn_y(t):
+            bank = passing_bank([P, S // BLOCK, P])
+            for b in range(S // BLOCK):
+                nc.tensor.transpose(bank[:, b, :], y_full[t][:, b * BLOCK : (b + 1) * BLOCK], ident[:])
+            nc.scalar.copy(y_turned[:, t], bank[:])
+
+        trial = [psum.tile([P, PACK, BLOCK], F32, name="trial", tag="bank%d" % b) for b in range(S // BLOCK)]
+        sig = [keep.tile([P, half // LINE, PACK, LINE], F32, name="sig%d" % h) for h in range(2)]
+
+        units = [(0, 0, half), (0, half, half), (1, 0, half), (2, 0, half), (3, 0, half), (1, half, half), (2, half, half)]
+        units.extend([(3, half, BLOCK), (3, half + BLOCK, BLOCK)])
+        partial = {}
+
+        def look_up(u, stage):
+            t, start, width = units[u]
             entries = slice(start // 16, (start + width) // 16)
-            step_t = psum.tile([P, blocks, len(part), P], F32, name="step_t", tag="bank%d" % step_bank)
-            for at, t in enumerate(part):
-                picked = []
-                for n in range(3):
-                    tile = ring.tile([P, width], F32, name="picked", bufs=GATHER_BUFS)
-                    nc.vector.tensor_scalar(
-                        tile[:], neg_y[t][:].indirect(lists[n][:, entries]), factors[n], 0.0, ALU.mult, ALU.add
-                    )
-                    picked.append(tile)
-                for b in range(blocks):
-                    first = start + b * BLOCK
-                    terms = [neg_y[t][:, first : first + BLOCK]]
-                    terms.extend(tile[:, b * BLOCK : (b + 1) * BLOCK] for tile in picked)
-                    for n, term in enumerate(terms):
-                        nc.tensor.matmul(
-                            step_t[:, b, at, :], term, ident[:], start=(n == 0), stop=(n == 3), is_transpose=True
-                        )
-            gain_t = ring.tile([P, blocks, len(part), P], F32, name="gain_t", bufs=3)
-            gain = psum.tile([P, len(part), width], F32, name="gain", tag="bank%d" % gain_bank)
+            window, offsets, op = ((y_half, r3_sb, ALU.add), (y_half, r2_sb, ALU.subtract), (y_full, r1_sb, ALU.add))[stage]
+            other = y_full[t][:, start : start + width] if stage == 0 else partial[u][:]
+            if (u, stage) == (len(units) - 1, 1):
+                result = keep.tile([P, width], F32, name="last_partial", tag="late", align_bytes=64)
+            else:
+                result = ring.tile([P, width], F32, name="picked", bufs=GATHER_BUFS)
+            nc.vector.tensor_tensor(result[:], window[t][:].indirect(offsets[:, entries]), other, op)
+            partial[u] = result
+
+        gains_t = {}
+
+        def scale_step(u):
+            t, start, width = units[u]
+            blocks = width // BLOCK
+            step_t = passing_bank([P, blocks, P])
             for b in range(blocks):
-                column = start // BLOCK + b
-                nc.scalar.activation(gain_t[:, b], step_t[:, b], ACT.Copy, scale=cr_sb[:, column : column + 1])
-                for at in range(len(part)):
-                    nc.tensor.transpose(gain[:, at, b * BLOCK : (b + 1) * BLOCK], gain_t[:, b, at, :], ident[:])
-            return gain
+                nc.tensor.transpose(step_t[:, b, :], partial[u][:, b * BLOCK : (b + 1) * BLOCK], ident[:])
+            gain_t = ring.tile([P, blocks, P], F32, name="gain_t", bufs=4)
+            for b in range(blocks):
+                block = start // BLOCK + b
+                nc.scalar.activation(gain_t[:, b], step_t[:, b], ACT.Copy, scale=cr_sb[:, block : block + 1])
+            gains_t[u] = gain_t
 
-        sig = keep.tile([P, S // LINE, PACK, LINE], F32)
-
-        def blend(start, width, part, gain, trial, trial_start):
-            groups = slice(start // LINE, (start + width) // LINE)
+        def turn_back(u):
+            t, start, width = units[u]
+            blocks = width // BLOCK
+            gain = passing_bank([P, width])
+            for b in range(blocks):
+                nc.tensor.transpose(gain[:, b * BLOCK : (b + 1) * BLOCK], gains_t[u][:, b, :], ident[:])
+            for b in range(blocks):
+                block = start // BLOCK + b
+                for n, term in enumerate((y_turned[:, t, block, :], gains_t[u][:, b, :])):
+                    nc.tensor.matmul(trial[block][:, t, :], term, ident[:], start=(n == 0), stop=(n == 1), is_transpose=True)
+            groups = slice(start % half // LINE, (start % half + width) // LINE)
             nc.scalar.activation(
-                sig[:, groups, part[0] : part[-1] + 1, :], gain[:].rearrange("p t (c i) -> p c t i", i=LINE), ACT.Sigmoid
+                sig[start // half][:, groups, t, :], gain[:].rearrange("p (c i) -> p c i", i=LINE), ACT.Sigmoid, scale=inv_gs[:, t : t + 1]
             )
-            for at, t in enumerate(part):
-                nc.vector.scalar_tensor_tensor(
-                    trial[:, groups, t, :],
-                    gain[:, at, :].rearrange("p (c i) -> p c i", i=LINE),
-                    gs_sb[:, t : t + 1],
-                    gs_y[:, t, start : start + width].rearrange("p (c i) -> p c i", i=LINE),
-                    ALU.mult,
-                    ALU.add,
-                )
 
-        def weigh(start, width, trial, trial_start):
-            groups = slice(start // LINE, (start + width) // LINE)
-            z_bf = ring.tile([P, width // LINE, LINE, PACK], BF16, name="z_bf", align_bytes=64, bufs=3)
+        turned = set()
+        for wave in range(len(units) + 3):
+            for stage in range(3):
+                if 0 <= wave - stage < len(units):
+                    look_up(wave - stage, stage)
+            if 0 <= wave - 2 < len(units):
+                t = units[wave - 2][0]
+                if t not in turned:
+                    turn_y(t)
+                    turned.add(t)
+                scale_step(wave - 2)
+            if 0 <= wave - 3:
+                turn_back(wave - 3)
+
+        d_codes = keep.tile([P, H], U32, tag="late", align_bytes=64)
+        nc.vector.tensor_copy(d_codes[:], d_table[:].indirect(kq_sb[:]))
+
+        out_view = out.rearrange("(m p) j -> p m j", p=P)
+        groups = BLOCK // LINE
+
+        def weigh(block):
+            z_bf = ring.tile([P, groups, LINE, PACK], BF16, name="z_bf", align_bytes=64, bufs=4)
             nc.vector.tensor_tensor(
                 z_bf[:].rearrange("p c i t -> p c t i"),
-                trial[:, groups],
-                sig[:, groups],
+                trial[block][:].rearrange("p t (c i) -> p c t i", i=LINE),
+                sig[block // 2][:, block % 2 * groups : (block % 2 + 1) * groups],
                 ALU.mult,
             )
             return z_bf
 
-        def finish(start, width, z_bf, banks, last):
-            cols = slice(start, start + width)
-            z_codes = ring.tile([P, width], U32, name="z_codes", align_bytes=64, bufs=3)
-            z_plane = ring.tile([P, width], U8, name="z_plane", align_bytes=64, bufs=3)
+        def finish(block, z_bf, banks):
+            cols = slice(block * BLOCK, (block + 1) * BLOCK)
+            z_codes = ring.tile([P, BLOCK], U32, name="z_codes", align_bytes=64, bufs=4)
+            z_plane = ring.tile([P, BLOCK], U8, name="z_plane", align_bytes=64, bufs=4)
             nc.vector.quantize_mx(
                 out=z_codes[:].bitcast(FP8X4), scales=z_plane[:], in_=z_bf[:].rearrange("p c i t -> p (c i t)")
             )
-            per_bank = 2 if last else S // width
-            for m0 in range(0, H // P, per_bank):
-                acc = psum.tile([P, per_bank, width], F32, name="acc", tag="bank%d" % banks[m0 // per_bank])
+            per_bank = H // P // len(banks)
+            for n, bank_number in enumerate(banks):
+                acc = psum.tile([P, per_bank, BLOCK], F32, name="acc", tag="bank%d" % bank_number)
                 for m in range(per_bank):
-                    rows = slice((m0 + m) * P, (m0 + m + 1) * P)
+                    rows = slice((n * per_bank + m) * P, (n * per_bank + m + 1) * P)
                     nc.tensor.matmul_mx(
                         out=acc[:, m, :],
                         lhsT=d_codes[:, rows].bitcast(FP8X4),
@@ -206,38 +246,19 @@ def tile_picked_diffevo_none_p_kernel(
                         start=True,
                         stop=True,
                     )
-                result = ring.tile([P, per_bank, width], F32, name="result", bufs=5)
-                if last and m0 == 0:
+                result = ring.tile([P, per_bank, BLOCK], F32, name="result", bufs=5)
+                target = out_view[:, n * per_bank : (n + 1) * per_bank, cols]
+                if len(banks) > 1 and n == 0:
                     nc.vector.tensor_scalar(result[:], acc[:], 0.0625, None, ALU.mult)
-                    nc.sync.dma_start(out_view[:, m0 : m0 + per_bank, cols], result[:])
+                    nc.sync.dma_start(target, result[:])
                 else:
                     nc.scalar.activation(result[:], acc[:], ACT.Copy, scale=0.0625)
-                    queue = nc.scalar if last else nc.sync
-                    queue.dma_start(out_view[:, m0 : m0 + per_bank, cols], result[:])
+                    queue = nc.scalar if n > 0 else nc.sync
+                    queue.dma_start(target, result[:])
 
-        half = S // 2
-        first_trial = keep.tile([P, S // LINE, PACK, LINE], F32)
-        second_trial = first_trial
-        steps = [
-            (0, half, (0, 1)),
-            (0, half, (2, 3)),
-            (half, half, (0, 1)),
-            (half, half, (2,)),
-            (half, BLOCK, (3,)),
-            (half + BLOCK, BLOCK, (3,)),
-        ]
-        banks = [(5, 6), (7, 0), (1, 2), (3, 4), (5, 7), (1, 3)]
-        gains = [look_up(*step, *pair) for step, pair in zip(steps, banks)]
-        nc.vector.tensor_copy(d_codes[:], d_table[:].indirect(kq_sb[:]))
-        for n in range(2):
-            blend(*steps[n], gains[n], first_trial, 0)
-        blend(*steps[2], gains[2], second_trial, half)
-        z_first = weigh(0, half, first_trial, 0)
-        blend(*steps[3], gains[3], second_trial, half)
-        blend(*steps[4], gains[4], second_trial, half)
-        finish(0, half, z_first, (1, 5), False)
-        z_third = weigh(half, BLOCK, second_trial, half)
-        blend(*steps[5], gains[5], second_trial, half)
-        finish(half, BLOCK, z_third, (6,), False)
-        z_fourth = weigh(half + BLOCK, BLOCK, second_trial, half)
-        finish(half + BLOCK, BLOCK, z_fourth, (0, 2), True)
+        out_banks = ((4,), (5,), (6,), (7, 0))
+        weighed = [weigh(0)]
+        for block in range(S // BLOCK):
+            if block + 1 < S // BLOCK:
+                weighed.append(weigh(block + 1))
+            finish(block, weighed[block], out_banks[block])

@@ -20,8 +20,8 @@ P = 128
 PACK = 4
 BLOCK = 128
 LINE = 4
-GATHER_BUFS = 27
-W_SPLIT = 176
+GATHER_BUFS = 29
+W_SPLIT = 256
 
 
 def tile_picked_diffevo_none_p_kernel(
@@ -84,19 +84,23 @@ def tile_picked_diffevo_none_p_kernel(
             )
         w_codes = keep.tile([P, PACK, P], U32, align_bytes=64)
         w_plane = keep.tile([P, PACK, P], U8, align_bytes=64)
-        for t in range(PACK):
+
+        def quantize_w(t):
             nc.vector.quantize_mx(
                 out=w_codes[:, t, :].bitcast(FP8X4),
                 scales=w_plane[:, t, :],
                 in_=w_bf[:, t, :, :].rearrange("p m j -> p (m j)"),
             )
 
+        quantize_w(0)
         half = S // 2
         x_codes = keep.tile([P, S], U32, align_bytes=64)
         nc.vector.tensor_copy(x_codes[:, :half], x_table[:].indirect(offs_sb[:, : half // 16]))
         half_gs = keep.tile([P, PACK], F32)
         nc.vector.tensor_scalar(half_gs[:], gs_sb[:], 0.5, None, ALU.mult)
         nc.vector.tensor_copy(x_codes[:, half:], x_table[:].indirect(offs_sb[:, half // 16 :]))
+        for t in range(1, PACK):
+            quantize_w(t)
         safe_gs = keep.tile([P, PACK], F32)
         nc.vector.scalar_tensor_tensor(safe_gs[:], gs_sb[:], 0.0, gs_sb[:], ALU.is_equal, ALU.add)
         inv_gs = keep.tile([P, PACK], F32)
@@ -108,7 +112,6 @@ def tile_picked_diffevo_none_p_kernel(
         for t in range(PACK):
             y_full.append(keep.tile([P, S], F32, name="y_full%d" % t))
             y_half.append(keep.tile([P, S], F32, name="y_half%d" % t))
-            made = []
             for c0, c1, bank_number in [span[1:] for span in y_spans if span[0] == t]:
                 bank = psum.tile([P, c1 - c0], F32, name="y_bank", tag="bank%d" % bank_number)
                 nc.tensor.matmul_mx(
@@ -120,12 +123,7 @@ def tile_picked_diffevo_none_p_kernel(
                     start=True,
                     stop=True,
                 )
-                if c0 > 0:
-                    nc.vector.tensor_scalar(y_half[t][:, c0:c1], bank[:], half_gs[:, t : t + 1], None, ALU.mult)
-                else:
-                    nc.scalar.activation(y_half[t][:, c0:c1], bank[:], ACT.Copy, scale=half_gs[:, t : t + 1])
-                made.append((c0, c1, bank))
-            for c0, c1, bank in made:
+                nc.scalar.activation(y_half[t][:, c0:c1], bank[:], ACT.Copy, scale=half_gs[:, t : t + 1])
                 nc.scalar.activation(y_full[t][:, c0:c1], bank[:], ACT.Copy, scale=gs_sb[:, t : t + 1])
 
         for r in range(4):
@@ -150,8 +148,8 @@ def tile_picked_diffevo_none_p_kernel(
         trial = [psum.tile([P, PACK, BLOCK], F32, name="trial", tag="bank%d" % b) for b in range(S // BLOCK)]
         sig = [keep.tile([P, half // LINE, PACK, LINE], F32, name="sig%d" % h) for h in range(2)]
 
-        units = [(0, 0, half), (0, half, half), (1, 0, half), (2, 0, half), (3, 0, half), (1, half, half), (2, half, half)]
-        units.extend([(3, half, BLOCK), (3, half + BLOCK, BLOCK)])
+        units = [(t, start, half) for t in range(PACK - 1) for start in (0, half)]
+        units.extend([(PACK - 1, start, BLOCK) for start in range(0, S, BLOCK)])
         partial = {}
 
         def look_up(u, stage):
@@ -195,19 +193,20 @@ def tile_picked_diffevo_none_p_kernel(
                 sig[start // half][:, groups, t, :], gain[:].rearrange("p (c i) -> p c i", i=LINE), ACT.Sigmoid, scale=inv_gs[:, t : t + 1]
             )
 
-        turned = set()
-        for wave in range(len(units) + 3):
-            for stage in range(3):
-                if 0 <= wave - stage < len(units):
-                    look_up(wave - stage, stage)
-            if 0 <= wave - 2 < len(units):
-                t = units[wave - 2][0]
-                if t not in turned:
-                    turn_y(t)
-                    turned.add(t)
-                scale_step(wave - 2)
-            if 0 <= wave - 3:
-                turn_back(wave - 3)
+        turn_y(0)
+        for t in range(PACK):
+            members = [u for u in range(len(units)) if units[u][0] == t]
+            if t + 1 < PACK:
+                turn_y(t + 1)
+            for wave in range(len(members) + 2):
+                for stage in range(3):
+                    if 0 <= wave - stage < len(members):
+                        look_up(members[wave - stage], stage)
+                if wave >= 2:
+                    scale_step(members[wave - 2])
+                if wave >= 3:
+                    turn_back(members[wave - 3])
+            turn_back(members[-1])
 
         d_codes = keep.tile([P, H], U32, tag="late", align_bytes=64)
         nc.vector.tensor_copy(d_codes[:], d_table[:].indirect(kq_sb[:]))
@@ -256,7 +255,7 @@ def tile_picked_diffevo_none_p_kernel(
                     queue = nc.scalar if n > 0 else nc.sync
                     queue.dma_start(target, result[:])
 
-        out_banks = ((4,), (5,), (6,), (7, 0))
+        out_banks = ((6,), (7,), (4,), (5, 0))
         weighed = [weigh(0)]
         for block in range(S // BLOCK):
             if block + 1 < S // BLOCK:

@@ -18,8 +18,10 @@ ALU = mybir.AluOpType
 
 P = 128
 PACK = 4
+STRIPE = 16
 BLOCK = 128
-LINE = 4
+HALF = S // 2
+RUN = 2
 GATHER_BUFS = 29
 W_SPLIT = 256
 
@@ -34,7 +36,7 @@ def tile_picked_diffevo_none_p_kernel(
         psum = ctx.enter_context(tc.psum_pool(name="psum", bufs=1))
 
         def load_list(src, name):
-            tile = keep.tile([P, S // 16], U16, name=name)
+            tile = keep.tile([P, S // STRIPE], U16, name=name)
             nc.sync.dma_start(tile[:], src)
             return tile
 
@@ -93,12 +95,11 @@ def tile_picked_diffevo_none_p_kernel(
             )
 
         quantize_w(0)
-        half = S // 2
         x_codes = keep.tile([P, S], U32, align_bytes=64)
-        nc.vector.tensor_copy(x_codes[:, :half], x_table[:].indirect(offs_sb[:, : half // 16]))
+        nc.vector.tensor_copy(x_codes[:, :HALF], x_table[:].indirect(offs_sb[:, : HALF // STRIPE]))
         half_gs = keep.tile([P, PACK], F32)
         nc.vector.tensor_scalar(half_gs[:], gs_sb[:], 0.5, None, ALU.mult)
-        nc.vector.tensor_copy(x_codes[:, half:], x_table[:].indirect(offs_sb[:, half // 16 :]))
+        nc.vector.tensor_copy(x_codes[:, HALF:], x_table[:].indirect(offs_sb[:, HALF // STRIPE :]))
         for t in range(1, PACK):
             quantize_w(t)
         safe_gs = keep.tile([P, PACK], F32)
@@ -106,13 +107,13 @@ def tile_picked_diffevo_none_p_kernel(
         inv_gs = keep.tile([P, PACK], F32)
         nc.vector.reciprocal(inv_gs[:], safe_gs[:])
 
+        y_spans = (((0, HALF, 4), (HALF, S, 5)), ((0, S, 0),), ((0, S, 1),), ((0, S, 2),))
         y_full = []
         y_half = []
-        y_spans = [(0, 0, half, 4), (0, half, S, 5), (1, 0, S, 0), (2, 0, S, 1), (3, 0, S, 2)]
         for t in range(PACK):
             y_full.append(keep.tile([P, S], F32, name="y_full%d" % t))
             y_half.append(keep.tile([P, S], F32, name="y_half%d" % t))
-            for c0, c1, bank_number in [span[1:] for span in y_spans if span[0] == t]:
+            for c0, c1, bank_number in y_spans[t]:
                 bank = psum.tile([P, c1 - c0], F32, name="y_bank", tag="bank%d" % bank_number)
                 nc.tensor.matmul_mx(
                     out=bank[:],
@@ -146,28 +147,29 @@ def tile_picked_diffevo_none_p_kernel(
             nc.scalar.copy(y_turned[:, t], bank[:])
 
         trial = [psum.tile([P, PACK, BLOCK], F32, name="trial", tag="bank%d" % b) for b in range(S // BLOCK)]
-        sig = [keep.tile([P, half // LINE, PACK, LINE], F32, name="sig%d" % h) for h in range(2)]
+        sig = [keep.tile([P, HALF // BLOCK, PACK, BLOCK], F32, name="sig%d" % h) for h in range(S // HALF)]
 
-        units = [(t, start, half) for t in range(PACK - 1) for start in (0, half)]
+        units = [(t, start, HALF) for t in range(PACK - 1) for start in (0, HALF)]
         units.extend([(PACK - 1, start, BLOCK) for start in range(0, S, BLOCK)])
+        stages = ((y_half, r3_sb, ALU.add), (y_half, r2_sb, ALU.subtract), (y_full, r1_sb, ALU.add))
         partial = {}
 
         def look_up(u, stage):
             t, start, width = units[u]
-            entries = slice(start // 16, (start + width) // 16)
-            window, offsets, op = ((y_half, r3_sb, ALU.add), (y_half, r2_sb, ALU.subtract), (y_full, r1_sb, ALU.add))[stage]
+            windows, offsets, op = stages[stage]
+            entries = slice(start // STRIPE, (start + width) // STRIPE)
             other = y_full[t][:, start : start + width] if stage == 0 else partial[u][:]
-            if (u, stage) == (len(units) - 1, 1):
+            if (u, stage) == (len(units) - 1, len(stages) - 2):
                 result = keep.tile([P, width], F32, name="last_partial", tag="late", align_bytes=64)
             else:
                 result = ring.tile([P, width], F32, name="picked", bufs=GATHER_BUFS)
-            nc.vector.tensor_tensor(result[:], window[t][:].indirect(offsets[:, entries]), other, op)
+            nc.vector.tensor_tensor(result[:], windows[t][:].indirect(offsets[:, entries]), other, op)
             partial[u] = result
 
         gains_t = {}
 
         def scale_step(u):
-            t, start, width = units[u]
+            start, width = units[u][1:]
             blocks = width // BLOCK
             step_t = passing_bank([P, blocks, P])
             for b in range(blocks):
@@ -187,10 +189,15 @@ def tile_picked_diffevo_none_p_kernel(
             for b in range(blocks):
                 block = start // BLOCK + b
                 for n, term in enumerate((y_turned[:, t, block, :], gains_t[u][:, b, :])):
-                    nc.tensor.matmul(trial[block][:, t, :], term, ident[:], start=(n == 0), stop=(n == 1), is_transpose=True)
-            groups = slice(start % half // LINE, (start % half + width) // LINE)
+                    nc.tensor.matmul(
+                        trial[block][:, t, :], term, ident[:], start=(n == 0), stop=(n == 1), is_transpose=True
+                    )
+            first = start % HALF // BLOCK
             nc.scalar.activation(
-                sig[start // half][:, groups, t, :], gain[:].rearrange("p (c i) -> p c i", i=LINE), ACT.Sigmoid, scale=inv_gs[:, t : t + 1]
+                sig[start // HALF][:, first : first + blocks, t, :],
+                gain[:].rearrange("p (b j) -> p b j", j=BLOCK),
+                ACT.Sigmoid,
+                scale=inv_gs[:, t : t + 1],
             )
 
         turn_y(0)
@@ -198,36 +205,37 @@ def tile_picked_diffevo_none_p_kernel(
             members = [u for u in range(len(units)) if units[u][0] == t]
             if t + 1 < PACK:
                 turn_y(t + 1)
-            for wave in range(len(members) + 2):
-                for stage in range(3):
+            for wave in range(len(members) + len(stages) - 1):
+                for stage in range(len(stages)):
                     if 0 <= wave - stage < len(members):
                         look_up(members[wave - stage], stage)
-                if wave >= 2:
-                    scale_step(members[wave - 2])
-                if wave >= 3:
-                    turn_back(members[wave - 3])
+                done = wave - (len(stages) - 1)
+                if done >= 0:
+                    scale_step(members[done])
+                if done >= 1:
+                    turn_back(members[done - 1])
             turn_back(members[-1])
 
         d_codes = keep.tile([P, H], U32, tag="late", align_bytes=64)
         nc.vector.tensor_copy(d_codes[:], d_table[:].indirect(kq_sb[:]))
 
         out_view = out.rearrange("(m p) j -> p m j", p=P)
-        groups = BLOCK // LINE
+        blocks_in_half = HALF // BLOCK
 
         def weigh(block):
-            z_bf = ring.tile([P, groups, LINE, PACK], BF16, name="z_bf", align_bytes=64, bufs=4)
+            z_bf = ring.tile([P, BLOCK // RUN, RUN, PACK], BF16, name="z_bf", align_bytes=64, bufs=S // BLOCK)
             nc.vector.tensor_tensor(
                 z_bf[:].rearrange("p c i t -> p c t i"),
-                trial[block][:].rearrange("p t (c i) -> p c t i", i=LINE),
-                sig[block // 2][:, block % 2 * groups : (block % 2 + 1) * groups],
+                trial[block][:].rearrange("p t (c i) -> p c t i", i=RUN),
+                sig[block // blocks_in_half][:, block % blocks_in_half].rearrange("p t (c i) -> p c t i", i=RUN),
                 ALU.mult,
             )
             return z_bf
 
         def finish(block, z_bf, banks):
             cols = slice(block * BLOCK, (block + 1) * BLOCK)
-            z_codes = ring.tile([P, BLOCK], U32, name="z_codes", align_bytes=64, bufs=4)
-            z_plane = ring.tile([P, BLOCK], U8, name="z_plane", align_bytes=64, bufs=4)
+            z_codes = ring.tile([P, BLOCK], U32, name="z_codes", align_bytes=64, bufs=S // BLOCK)
+            z_plane = ring.tile([P, BLOCK], U8, name="z_plane", align_bytes=64, bufs=S // BLOCK)
             nc.vector.quantize_mx(
                 out=z_codes[:].bitcast(FP8X4), scales=z_plane[:], in_=z_bf[:].rearrange("p c i t -> p (c i t)")
             )
@@ -245,7 +253,7 @@ def tile_picked_diffevo_none_p_kernel(
                         start=True,
                         stop=True,
                     )
-                result = ring.tile([P, per_bank, BLOCK], F32, name="result", bufs=5)
+                result = ring.tile([P, per_bank, BLOCK], F32, name="result", bufs=S // BLOCK + 1)
                 target = out_view[:, n * per_bank : (n + 1) * per_bank, cols]
                 if len(banks) > 1 and n == 0:
                     nc.vector.tensor_scalar(result[:], acc[:], 0.0625, None, ALU.mult)

from contextlib import ExitStack

import concourse.mybir as mybir
from concourse.masks import make_identity

K, T, S, H, G = 512, 2048, 512, 512, 2048
FLOPS = 2 * K * H * S + 2 * H * H * S

F32 = mybir.dt.float32
BF16 = mybir.dt.bfloat16
I32 = mybir.dt.int32
U32 = mybir.dt.uint32
U16 = mybir.dt.uint16
U8 = mybir.dt.uint8
FP8X4 = mybir.dt.float8_e4m3fn_x4
ACT = mybir.ActivationFunctionType
ALU = mybir.AluOpType

P = 128
PACK = 4
STRIPE = 16
BLOCK = 128
HALF = S // 2
RUN = 2
GATHER_BUFS = 29
W_SPLIT = 256


def tile_picked_diffevo_none_p_kernel(
    tc, x_words, x_scales, w1, cr, gs, d_words, d_scales, offs, r1, r2, r3, kq, out
):
    nc = tc.nc
    with ExitStack() as ctx:
        keep = ctx.enter_context(tc.tile_pool(name="keep", bufs=1))
        ring = ctx.enter_context(tc.tile_pool(name="ring", bufs=2))
        psum = ctx.enter_context(tc.psum_pool(name="psum", bufs=1))

        def load_list(src, name):
            tile = keep.tile([P, S // STRIPE], U16, name=name)
            nc.sync.dma_start(tile[:], src)
            return tile

        d_scale_table = keep.tile([P, G], U8, align_bytes=64)
        nc.gpsimd.memset(d_scale_table[:].bitcast(I32), 0)
        x_scale_table = keep.tile([P, T], U8, align_bytes=64)
        nc.vector.memset(x_scale_table[:].bitcast(I32), 0)
        warm = keep.tile([P, 8], F32)
        nc.vector.memset(warm[:], 0.0)
        nc.scalar.activation(warm[:, 0:1], warm[:, 1:2], ACT.Sigmoid)
        d_scale_plane = keep.tile([P, H], U8, align_bytes=64)
        nc.gpsimd.memset(d_scale_plane[:].bitcast(I32), 0)
        ident = keep.tile([P, P], F32)
        make_identity(nc, ident[:])

        offs_sb = load_list(offs, "offs_sb")
        kq_sb = load_list(kq, "kq_sb")
        nc.sync.dma_start(d_scale_table[0:P:8, :].bitcast(I32), d_scales[0].bitcast(I32))
        x_scale_rows = x_scales[0].rearrange("(q r) n -> r q n", r=4)
        for r in range(4):
            nc.sync.dma_start(x_scale_table[r:P:32, :].bitcast(I32), x_scale_rows[r].bitcast(I32))
        w_raw = keep.tile([P, PACK, H], F32)
        nc.sync.dma_start(w_raw[:], w1.rearrange("(p j) c -> p j c", j=PACK))
        x_table = keep.tile([P, T], U32, align_bytes=64)
        nc.sync.dma_start(x_table[:].bitcast(I32), x_words[0].rearrange("p n t -> p (n t)").bitcast(I32))
        gs_sb = keep.tile([P, PACK], F32)
        nc.sync.dma_start(gs_sb[:], gs.rearrange("(p t) o -> p (t o)", t=PACK))
        r3_sb = load_list(r3, "r3_sb")
        r2_sb = load_list(r2, "r2_sb")
        r1_sb = load_list(r1, "r1_sb")
        cr_sb = keep.tile([P, S // BLOCK], F32)
        with nc.allow_non_contiguous_dma(reason="one value of cr for each partition and block"):
            nc.sync.dma_start(cr_sb[:], cr[0].rearrange("(b p) -> p b", p=P))
        d_table = keep.tile([P, G], U32, align_bytes=64)
        nc.sync.dma_start(d_table[:].bitcast(I32), d_words[0].rearrange("p n t -> p (n t)").bitcast(I32))

        d_picked_scales = keep.tile([P, H], U8, align_bytes=64)
        nc.vector.tensor_copy(d_picked_scales[:], d_scale_table[:].indirect(kq_sb[:]))
        x_plane = keep.tile([P, S], U8, align_bytes=64)
        nc.vector.tensor_copy(x_plane[:], x_scale_table[:].indirect(offs_sb[:]))

        w_bf = keep.tile([P, PACK, P, PACK], BF16, align_bytes=64)
        for c0, c1, engine_copy in ((0, W_SPLIT, nc.scalar.copy), (W_SPLIT, H, nc.vector.tensor_copy)):
            engine_copy(
                w_bf[:, :, c0 // PACK : c1 // PACK, :].rearrange("p t m j -> p m j t"),
                w_raw[:, :, c0:c1].rearrange("p j (m t) -> p m j t", t=PACK),
            )
        w_codes = keep.tile([P, PACK, P], U32, align_bytes=64)
        w_plane = keep.tile([P, PACK, P], U8, align_bytes=64)

        def quantize_w(t):
            nc.vector.quantize_mx(
                out=w_codes[:, t, :].bitcast(FP8X4),
                scales=w_plane[:, t, :],
                in_=w_bf[:, t, :, :].rearrange("p m j -> p (m j)"),
            )

        quantize_w(0)
        x_codes = keep.tile([P, S], U32, align_bytes=64)
        nc.vector.tensor_copy(x_codes[:, :HALF], x_table[:].indirect(offs_sb[:, : HALF // STRIPE]))
        half_gs = keep.tile([P, PACK], F32)
        nc.vector.tensor_scalar(half_gs[:], gs_sb[:], 0.5, None, ALU.mult)
        nc.vector.tensor_copy(x_codes[:, HALF:], x_table[:].indirect(offs_sb[:, HALF // STRIPE :]))
        for t in range(1, PACK):
            quantize_w(t)
        safe_gs = keep.tile([P, PACK], F32)
        nc.vector.scalar_tensor_tensor(safe_gs[:], gs_sb[:], 0.0, gs_sb[:], ALU.is_equal, ALU.add)
        inv_gs = keep.tile([P, PACK], F32)
        nc.vector.reciprocal(inv_gs[:], safe_gs[:])

        y_spans = (((0, HALF, 4), (HALF, S, 5)), ((0, S, 0),), ((0, S, 1),), ((0, S, 2),))
        y_full = []
        y_half = []
        for t in range(PACK):
            y_full.append(keep.tile([P, S], F32, name="y_full%d" % t))
            y_half.append(keep.tile([P, S], F32, name="y_half%d" % t))
            for c0, c1, bank_number in y_spans[t]:
                bank = psum.tile([P, c1 - c0], F32, name="y_bank", tag="bank%d" % bank_number)
                nc.tensor.matmul_mx(
                    out=bank[:],
                    lhsT=w_codes[:, t, :].bitcast(FP8X4),
                    lhsT_scale=w_plane[:, t, :],
                    rhs=x_codes[:, c0:c1].bitcast(FP8X4),
                    rhs_scale=x_plane[:, c0:c1],
                    start=True,
                    stop=True,
                )
                nc.scalar.activation(y_half[t][:, c0:c1], bank[:], ACT.Copy, scale=half_gs[:, t : t + 1])
                nc.scalar.activation(y_full[t][:, c0:c1], bank[:], ACT.Copy, scale=gs_sb[:, t : t + 1])

        for r in range(4):
            nc.sync.dma_start(
                d_scale_plane[r:P:32, :].bitcast(I32), d_picked_scales[8 * r : P : 32, :].bitcast(I32)
            )

        y_turned = keep.tile([P, PACK, S // BLOCK, P], F32)
        taken = []

        def passing_bank(shape):
            bank = psum.tile(shape, F32, name="passing", tag="bank%d" % (4 + (len(taken) + 2) % 4))
            taken.append(bank)
            return bank

        def turn_y(t):
            bank = passing_bank([P, S // BLOCK, P])
            for b in range(S // BLOCK):
                nc.tensor.transpose(bank[:, b, :], y_full[t][:, b * BLOCK : (b + 1) * BLOCK], ident[:])
            nc.scalar.copy(y_turned[:, t], bank[:])

        trial = [psum.tile([P, PACK, BLOCK], F32, name="trial", tag="bank%d" % b) for b in range(S // BLOCK)]
        sig = [keep.tile([P, HALF // BLOCK, PACK, BLOCK], F32, name="sig%d" % h) for h in range(S // HALF)]

        units = [(t, start, HALF) for t in range(PACK - 1) for start in (0, HALF)]
        units.extend([(PACK - 1, start, BLOCK) for start in range(0, S, BLOCK)])
        stages = ((y_half, r3_sb, ALU.add), (y_half, r2_sb, ALU.subtract), (y_full, r1_sb, ALU.add))
        partial = {}

        def look_up(u, stage):
            t, start, width = units[u]
            windows, offsets, op = stages[stage]
            entries = slice(start // STRIPE, (start + width) // STRIPE)
            other = y_full[t][:, start : start + width] if stage == 0 else partial[u][:]
            if (u, stage) == (len(units) - 1, len(stages) - 2):
                result = keep.tile([P, width], F32, name="last_partial", tag="late", align_bytes=64)
            else:
                result = ring.tile([P, width], F32, name="picked", bufs=GATHER_BUFS)
            nc.vector.tensor_tensor(result[:], windows[t][:].indirect(offsets[:, entries]), other, op)
            partial[u] = result

        gains_t = {}

        def scale_step(u):
            start, width = units[u][1:]
            blocks = width // BLOCK
            step_t = passing_bank([P, blocks, P])
            for b in range(blocks):
                nc.tensor.transpose(step_t[:, b, :], partial[u][:, b * BLOCK : (b + 1) * BLOCK], ident[:])
            gain_t = ring.tile([P, blocks, P], F32, name="gain_t", bufs=4)
            for b in range(blocks):
                block = start // BLOCK + b
                nc.scalar.activation(gain_t[:, b], step_t[:, b], ACT.Copy, scale=cr_sb[:, block : block + 1])
            gains_t[u] = gain_t

        def turn_back(u):
            t, start, width = units[u]
            blocks = width // BLOCK
            gain = passing_bank([P, width])
            for b in range(blocks):
                nc.tensor.transpose(gain[:, b * BLOCK : (b + 1) * BLOCK], gains_t[u][:, b, :], ident[:])
            for b in range(blocks):
                block = start // BLOCK + b
                for n, term in enumerate((y_turned[:, t, block, :], gains_t[u][:, b, :])):
                    nc.tensor.matmul(
                        trial[block][:, t, :], term, ident[:], start=(n == 0), stop=(n == 1), is_transpose=True
                    )
            first = start % HALF // BLOCK
            nc.scalar.activation(
                sig[start // HALF][:, first : first + blocks, t, :],
                gain[:].rearrange("p (b j) -> p b j", j=BLOCK),
                ACT.Sigmoid,
                scale=inv_gs[:, t : t + 1],
            )

        turn_y(0)
        for t in range(PACK):
            members = [u for u in range(len(units)) if units[u][0] == t]
            if t + 1 < PACK:
                turn_y(t + 1)
            for wave in range(len(members) + len(stages) - 1):
                for stage in range(len(stages)):
                    if 0 <= wave - stage < len(members):
                        look_up(members[wave - stage], stage)
                done = wave - (len(stages) - 1)
                if done >= 0:
                    scale_step(members[done])
                if done >= 1:
                    turn_back(members[done - 1])
            turn_back(members[-1])

        d_codes = keep.tile([P, H], U32, tag="late", align_bytes=64)
        nc.vector.tensor_copy(d_codes[:], d_table[:].indirect(kq_sb[:]))

        out_view = out.rearrange("(m p) j -> p m j", p=P)
        blocks_in_half = HALF // BLOCK

        def weigh(block):
            z_bf = ring.tile([P, BLOCK // RUN, RUN, PACK], BF16, name="z_bf", align_bytes=64, bufs=S // BLOCK)
            nc.vector.tensor_tensor(
                z_bf[:].rearrange("p c i t -> p c t i"),
                trial[block][:].rearrange("p t (c i) -> p c t i", i=RUN),
                sig[block // blocks_in_half][:, block % blocks_in_half].rearrange("p t (c i) -> p c t i", i=RUN),
                ALU.mult,
            )
            return z_bf

        def finish(block, z_bf, banks):
            cols = slice(block * BLOCK, (block + 1) * BLOCK)
            z_codes = ring.tile([P, BLOCK], U32, name="z_codes", align_bytes=64, bufs=S // BLOCK)
            z_plane = ring.tile([P, BLOCK], U8, name="z_plane", align_bytes=64, bufs=S // BLOCK)
            nc.vector.quantize_mx(
                out=z_codes[:].bitcast(FP8X4), scales=z_plane[:], in_=z_bf[:].rearrange("p c i t -> p (c i t)")
            )
            per_bank = H // P // len(banks)
            for n, bank_number in enumerate(banks):
                acc = psum.tile([P, per_bank, BLOCK], F32, name="acc", tag="bank%d" % bank_number)
                for m in range(per_bank):
                    rows = slice((n * per_bank + m) * P, (n * per_bank + m + 1) * P)
                    nc.tensor.matmul_mx(
                        out=acc[:, m, :],
                        lhsT=d_codes[:, rows].bitcast(FP8X4),
                        lhsT_scale=d_scale_plane[:, rows],
                        rhs=z_codes[:].bitcast(FP8X4),
                        rhs_scale=z_plane[:],
                        start=True,
                        stop=True,
                    )
                result = ring.tile([P, per_bank, BLOCK], F32, name="result", bufs=S // BLOCK + 1)
                target = out_view[:, n * per_bank : (n + 1) * per_bank, cols]
                if len(banks) > 1 and n == 0:
                    nc.vector.tensor_scalar(result[:], acc[:], 0.0625, None, ALU.mult)
                    nc.sync.dma_start(target, result[:])
                else:
                    nc.scalar.activation(result[:], acc[:], ACT.Copy, scale=0.0625)
                    queue = nc.scalar if n > 0 else nc.sync
                    queue.dma_start(target, result[:])

        out_banks = ((6,), (7,), (4,), (5, 0))
        weighed = [weigh(0)]
        for block in range(S // BLOCK):
            if block + 1 < S // BLOCK:
                weighed.append(weigh(block + 1))
            finish(block, weighed[block], out_banks[block])
